import numpy as np
import ml_dtypes


def mxq(x, axis, fmt="e4m3"):
    dtype, down = {"e4m3": (ml_dtypes.float8_e4m3fn, 7), "e5m2": (ml_dtypes.float8_e5m2, 14)}[fmt]
    v = np.moveaxis(np.asarray(x, np.float32).astype(ml_dtypes.bfloat16).astype(np.float64), axis, -1)
    blocks = v.reshape(v.shape[:-1] + (-1, 32))
    amax = np.abs(blocks).max(-1, keepdims=True)
    byte = np.maximum(np.where(amax > 0, np.frexp(amax)[1] - 1 + 127, 0) - down, 1)
    scale = np.exp2(byte - 127.0)
    codes = (blocks / scale).astype(np.float32).astype(dtype).astype(np.float64)
    return np.moveaxis((codes * scale).reshape(v.shape), -1, axis)


WIDE = False


def mx_kscale(k):
    if not WIDE:
        return np.ones(k)
    levels = np.array([24, -24, 12, -12, 0])
    if k % 512:
        return np.exp2(np.random.permutation(np.resize(levels, k // 32))).repeat(32)
    a = np.empty((k // 512, 16))
    for p in range(k // 512):
        a[p, :8] = np.random.permutation(np.resize(levels, 8))
        for g in range(8):
            far = levels[np.abs(levels - a[p, g]) >= 10]
            a[p, g + 8] = far[np.random.randint(len(far))]
    return np.exp2(a.ravel()).repeat(32)


def f64(x):
    return np.asarray(x).astype(np.float64)


def striped8(idx):
    return np.concatenate([v.reshape(-1, 16).T for v in idx]).astype(np.uint16)


def unstriped8(offs):
    return np.stack([offs[16 * g:16 * g + 16].T.reshape(-1) for g in range(8)]).astype(np.int64)


E2M1 = np.array([0.0, 0.5, 1.0, 1.5, 2.0, 3.0, 4.0, 6.0, -0.0, -0.5, -1.0, -1.5, -2.0, -3.0, -4.0, -6.0])


def pack_weight(w, fmt):
    k, n = w.shape
    w = f64(np.asarray(w, np.float32).astype(ml_dtypes.bfloat16)).reshape(k // 32, 32, n)
    amax = np.abs(w).max(1)
    if fmt == "e4m3":
        byte = np.frexp(amax)[1] - 1 + 127 - 7
    else:
        mant, ex = np.frexp(amax / 6.0)
        byte = np.where(mant > 0.5, ex, ex - 1) + 127
    byte = np.clip(np.where(amax > 0, byte, 1), 1, 254)
    scaled = (w * np.exp2(127.0 - byte)[:, None, :]).reshape(k, n).astype(np.float32)
    by_word = np.ascontiguousarray(scaled.reshape(k // 512, 128, 4, n).transpose(0, 1, 3, 2))
    if fmt == "e4m3":
        words = by_word.astype(ml_dtypes.float8_e4m3fn).view(np.uint8)
    else:
        c = by_word.astype(ml_dtypes.float4_e2m1fn).view(np.uint8) & 0xF
        words = (c[..., 0::2] | (c[..., 1::2] << 4)).reshape(k // 512, 128, 2 * n)
    return np.ascontiguousarray(words), np.ascontiguousarray(byte.astype(np.uint8).reshape(k // 512, 16, n))


def unpack_weight(words, scales, fmt):
    g, _, n = scales.shape
    words = np.ascontiguousarray(words).reshape(g, 128, n, -1)
    if fmt == "e4m3":
        vals = words.view(ml_dtypes.float8_e4m3fn).astype(np.float64)
    else:
        nib = np.empty((g, 128, n, 4), np.uint8)
        nib[..., 0::2] = words & 0xF
        nib[..., 1::2] = words >> 4
        vals = E2M1[nib]
    vals = vals * np.repeat(np.exp2(scales.astype(np.float64) - 127.0), 8, axis=1)[..., None]
    return vals.transpose(0, 1, 3, 2).reshape(g * 512, n)


def silu(f):
    return f / (1.0 + np.exp(-np.maximum(f, -700.0)))


K, N, T, J = 512, 512, 2048, 512


def setup_inputs():
    n = np.random.standard_normal
    s = mx_kscale(K)[:, None]
    p_w = pack_weight(n((K, N)) / np.sqrt(K) / s, "e4m3")
    return {
        "xT": (n((K, T)) * s).astype(np.float32),
        "wgt": np.repeat(np.random.uniform(0.5, 2.0, (8, 2 * J)), 16, axis=0).astype(np.float32),
        "w_words": p_w[0],
        "w_scales": p_w[1],
        "iw0": (np.random.uniform(0.1, 0.9, (N, J))).astype(np.float32),
        "iw1": (np.random.uniform(0.1, 0.9, (N, J))).astype(np.float32),
        "b": (0.3 * n(N)).astype(np.float32),
        "offs": striped8(np.stack([np.concatenate([np.random.permutation(T)[:J] for _ in range(2)]) for _ in range(8)])),
    }


def reference(xT, wgt, w_words, w_scales, iw0, iw1, b, offs):
    idx = unstriped8(offs)
    rows = np.arange(K)
    xg = f64(wgt)[rows // 4 % 128] * f64(xT)[rows[:, None], idx[rows % 512 // 64]]
    xT_ = mxq(xg, 0, "e4m3").reshape(K, 2, J)
    w_ = unpack_weight(w_words, w_scales, "e4m3")
    a0 = w_.T @ xT_[:, 0]
    a1 = w_.T @ xT_[:, 1]
    return silu(a0 * f64(iw0) + a1 * f64(iw1) + f64(b)[:, None])

@@ -1,0 +1,128 @@
+from contextlib import ExitStack
+
+import concourse.mybir as mybir
+
+K, N, T, J = 512, 512, 2048, 512
+PICKS = 2
+FLOPS = 2 * K * N * J * PICKS
+
+F32 = mybir.dt.float32
+BF16 = mybir.dt.bfloat16
+I32 = mybir.dt.int32
+U32 = mybir.dt.uint32
+U16 = mybir.dt.uint16
+U8 = mybir.dt.uint8
+FP8X4 = mybir.dt.float8_e4m3fn_x4
+MULT = mybir.AluOpType.mult
+ADD = mybir.AluOpType.add
+SILU = mybir.ActivationFunctionType.Silu
+
+P = 128
+PACK = 4
+LIST_ROWS = 16
+HALVES = 2
+JH = J // HALVES
+N_TILES = N // P
+
+
+def tile_list_soft_silu_kernel(tc, xT, wgt, w_words, w_scales, iw0, iw1, b, offs, out):
+    nc = tc.nc
+    with ExitStack() as ctx:
+        keep = ctx.enter_context(tc.tile_pool(name="keep", bufs=1))
+        psum = ctx.enter_context(tc.psum_pool(name="psum", bufs=1))
+
+        offsets = keep.tile([P, PICKS * J // LIST_ROWS], U16, name="offsets")
+        nc.sync.dma_start(offsets[:], offs)
+        wgt_sb = [keep.tile([P, J], F32, name=f"wgt{c}") for c in range(PICKS)]
+        x_planes = xT.rearrange("(p i) t -> i p t", i=PACK)
+        x_sb = []
+        for i in range(PACK):
+            plane = keep.tile([P, T], F32, name=f"x_plane{i}")
+            nc.sync.dma_start(plane[:], x_planes[i])
+            x_sb.append(plane)
+            if i == 0:
+                for c in range(PICKS):
+                    nc.sync.dma_start(wgt_sb[c][:], wgt[:, c * J : (c + 1) * J])
+
+        w_codes = keep.tile([P, N], U32, name="w_codes", align_bytes=64)
+        nc.sync.dma_start(w_codes[:].bitcast(I32), w_words[0].rearrange("p n i -> p (n i)").bitcast(I32))
+        w_scale = keep.tile([P, N], U8, name="w_scale", align_bytes=64)
+        nc.gpsimd.memset(w_scale[:].bitcast(I32), 0)
+        for q in range(4):
+            nc.sync.dma_start(w_scale[32 * q : 32 * q + 4, :].bitcast(I32), w_scales[0, 4 * q : 4 * q + 4, :].bitcast(I32))
+
+        iw_sb = []
+        bias = keep.tile([P, N_TILES], F32, name="bias")
+        for h in range(HALVES):
+            both = keep.tile([P, PICKS, N_TILES, JH], F32, name=f"iw_half{h}")
+            for c, iw in enumerate((iw0, iw1)):
+                nc.sync.dma_start(both[:, c], iw[:, h * JH : (h + 1) * JH].rearrange("(t p) j -> p t j", p=P))
+            iw_sb.append(both)
+            if h == 0:
+                with nc.allow_non_contiguous_dma(reason="one bias value a partition"):
+                    nc.sync.dma_start(bias[:], b.rearrange("(t p) -> p t", p=P))
+
+        def gather(dst, i, first, count):
+            window = x_sb[i][:].indirect(offsets[:, first // LIST_ROWS : (first + count) // LIST_ROWS])
+            nc.vector.tensor_tensor(dst, window, wgt_sb[first // J][:, first % J : first % J + count], MULT)
+
+        chunks = [(h, c) for h in range(HALVES) for c in range(PICKS)]
+        low = [keep.tile([P, 2, J], F32, name=f"low{c}") for c in range(PICKS)]
+        high = {hc: keep.tile([P, 2, JH], F32, name=f"high{hc[0]}{hc[1]}") for hc in chunks}
+        woven = {hc: keep.tile([P, JH, PACK], BF16, name=f"woven{hc[0]}{hc[1]}", align_bytes=64) for hc in chunks}
+        codes = {hc: keep.tile([P, JH], U32, name=f"codes{hc[0]}{hc[1]}", align_bytes=64) for hc in chunks}
+        scale = {hc: keep.tile([P, JH], U8, name=f"scale{hc[0]}{hc[1]}", align_bytes=64) for hc in chunks}
+
+        for i in range(2):
+            for c in range(PICKS):
+                gather(low[c][:, i, :], i, c * J, J)
+        for c in range(PICKS):
+            for h in range(HALVES):
+                nc.scalar.copy(woven[h, c][:, :, 0:2], low[c][:, :, h * JH : (h + 1) * JH].rearrange("p i j -> p j i"))
+        for i in range(2, PACK):
+            for h, c in chunks:
+                gather(high[h, c][:, i - 2, :], i, c * J + h * JH, JH)
+        for h, c in chunks:
+            nc.scalar.copy(woven[h, c][:, :, 2:4], high[h, c][:].rearrange("p i j -> p j i"))
+
+        banks = {(h, t): psum.tile([P, PICKS, JH], F32, name=f"bank{h}{t}") for h in range(HALVES) for t in range(N_TILES)}
+
+        def quantise(h, c):
+            nc.vector.quantize_mx(
+                out=codes[h, c][:].bitcast(FP8X4), scales=scale[h, c][:], in_=woven[h, c][:].rearrange("p j i -> p (j i)")
+            )
+
+        def project(h, t):
+            cols = slice(t * P, (t + 1) * P)
+            for c in range(PICKS):
+                nc.tensor.matmul_mx(
+                    out=banks[h, t][:, c, :],
+                    lhsT=w_codes[:, cols].bitcast(FP8X4),
+                    lhsT_scale=w_scale[:, cols],
+                    rhs=codes[h, c][:].bitcast(FP8X4),
+                    rhs_scale=scale[h, c][:],
+                    start=True,
+                    stop=True,
+                )
+
+        def pool_and_store(h, t, adder, lo=0, hi=JH):
+            width = hi - lo
+            terms = keep.tile([P, PICKS, width], F32, name=f"terms{h}{t}{lo}")
+            nc.vector.tensor_tensor(terms[:], banks[h, t][:, :, lo:hi], iw_sb[h][:, :, t, lo:hi], MULT)
+            pooled = keep.tile([P, width], F32, name=f"pooled{h}{t}{lo}")
+            adder.tensor_tensor(pooled[:], terms[:, 0, :], terms[:, 1, :], ADD)
+            result = keep.tile([P, width], F32, name=f"result{h}{t}{lo}")
+            nc.scalar.activation(result[:], pooled[:], SILU, bias=bias[:, t : t + 1])
+            nc.sync.dma_start(out[t * P : (t + 1) * P, h * JH + lo : h * JH + hi], result[:])
+
+        for h, c in chunks:
+            quantise(h, c)
+        for h in range(HALVES):
+            for t in range(N_TILES):
+                project(h, t)
+        for t in range(N_TILES):
+            pool_and_store(0, t, nc.gpsimd)
+        pool_and_store(1, 0, nc.vector)
+        pool_and_store(1, 1, nc.gpsimd)
+        pool_and_store(1, 2, nc.vector)
+        pool_and_store(1, 3, nc.vector)

@@ -32,7 +32,6 @@ def tile_list_soft_silu_kernel(tc, xT, wgt, w_words, w_scales, iw0, iw1, b, offs
         psum = ctx.enter_context(tc.psum_pool(name="psum", bufs=1))
 
         offsets = keep.tile([P, PICKS * J // LIST_ROWS], U16, name="offsets")
-        nc.sync.dma_start(offsets[:], offs)
         wgt_sb = [keep.tile([P, J], F32, name=f"wgt{c}") for c in range(PICKS)]
         x_planes = xT.rearrange("(p i) t -> i p t", i=PACK)
         x_sb = []
@@ -41,6 +40,7 @@ def tile_list_soft_silu_kernel(tc, xT, wgt, w_words, w_scales, iw0, iw1, b, offs
             nc.sync.dma_start(plane[:], x_planes[i])
             x_sb.append(plane)
             if i == 0:
+                nc.sync.dma_start(offsets[:], offs)
                 for c in range(PICKS):
                     nc.sync.dma_start(wgt_sb[c][:], wgt[:, c * J : (c + 1) * J])
 
@@ -53,12 +53,12 @@ def tile_list_soft_silu_kernel(tc, xT, wgt, w_words, w_scales, iw0, iw1, b, offs
 
         iw_sb = []
         bias = keep.tile([P, N_TILES], F32, name="bias")
-        for h in range(HALVES):
-            both = keep.tile([P, PICKS, N_TILES, JH], F32, name=f"iw_half{h}")
+        for t in range(N_TILES):
+            both = keep.tile([P, PICKS, J], F32, name=f"iw_rows{t}")
             for c, iw in enumerate((iw0, iw1)):
-                nc.sync.dma_start(both[:, c], iw[:, h * JH : (h + 1) * JH].rearrange("(t p) j -> p t j", p=P))
+                nc.sync.dma_start(both[:, c, :], iw[t * P : (t + 1) * P, :])
             iw_sb.append(both)
-            if h == 0:
+            if t == 1:
                 with nc.allow_non_contiguous_dma(reason="one bias value a partition"):
                     nc.sync.dma_start(bias[:], b.rearrange("(t p) -> p t", p=P))
 
@@ -105,24 +105,34 @@ def tile_list_soft_silu_kernel(tc, xT, wgt, w_words, w_scales, iw0, iw1, b, offs
                     stop=True,
                 )
 
-        def pool_and_store(h, t, adder, lo=0, hi=JH):
-            width = hi - lo
-            terms = keep.tile([P, PICKS, width], F32, name=f"terms{h}{t}{lo}")
-            nc.vector.tensor_tensor(terms[:], banks[h, t][:, :, lo:hi], iw_sb[h][:, :, t, lo:hi], MULT)
-            pooled = keep.tile([P, width], F32, name=f"pooled{h}{t}{lo}")
-            adder.tensor_tensor(pooled[:], terms[:, 0, :], terms[:, 1, :], ADD)
-            result = keep.tile([P, width], F32, name=f"result{h}{t}{lo}")
+        def weigh(h, t):
+            terms = keep.tile([P, PICKS, JH], F32, name=f"terms{h}{t}")
+            nc.vector.tensor_tensor(terms[:], banks[h, t][:], iw_sb[t][:, :, h * JH : (h + 1) * JH], MULT)
+            return terms
+
+        def finish(t, pooled, cols, label):
+            result = keep.tile(list(pooled.shape), F32, name=f"result{label}")
             nc.scalar.activation(result[:], pooled[:], SILU, bias=bias[:, t : t + 1])
-            nc.sync.dma_start(out[t * P : (t + 1) * P, h * JH + lo : h * JH + hi], result[:])
+            nc.sync.dma_start(out[t * P : (t + 1) * P, cols], result[:])
 
         for h, c in chunks:
             quantise(h, c)
-        for h in range(HALVES):
-            for t in range(N_TILES):
-                project(h, t)
-        for t in range(N_TILES):
-            pool_and_store(0, t, nc.gpsimd)
-        pool_and_store(1, 0, nc.vector)
-        pool_and_store(1, 1, nc.gpsimd)
-        pool_and_store(1, 2, nc.vector)
-        pool_and_store(1, 3, nc.vector)
+        early = [(h, t) for h in range(HALVES) for t in range(2)]
+        late = [(h, t) for t in range(2, N_TILES) for h in range(HALVES)]
+        for h, t in early + late:
+            project(h, t)
+        pooled_rows = [keep.tile([P, J], F32, name=f"pooled{t}") for t in range(2)]
+        for h, t in early:
+            terms = weigh(h, t)
+            nc.gpsimd.tensor_tensor(pooled_rows[t][:, h * JH : (h + 1) * JH], terms[:, 0, :], terms[:, 1, :], ADD)
+            if h == HALVES - 1:
+                finish(t, pooled_rows[t], slice(0, J), f"{t}")
+
+        def pool_late(h, t, terms, adder):
+            pooled = keep.tile([P, JH], F32, name=f"pooled_late{h}{t}")
+            adder.tensor_tensor(pooled[:], terms[:, 0, :], terms[:, 1, :], ADD)
+            finish(t, pooled, slice(h * JH, (h + 1) * JH), f"_late{h}{t}")
+
+        late_terms = [weigh(h, t) for h, t in late]
+        for u, ((h, t), terms) in enumerate(zip(late, late_terms)):
+            pool_late(h, t, terms, nc.gpsimd if u == 0 else nc.vector)

@@ -1,6 +1,7 @@
 from contextlib import ExitStack
 
 import concourse.mybir as mybir
+from concourse.masks import make_identity
 
 K, N, T, J = 512, 512, 2048, 512
 PICKS = 2
@@ -20,6 +21,9 @@ SILU = mybir.ActivationFunctionType.Silu
 P = 128
 PACK = 4
 LIST_ROWS = 16
+HEADS = 8
+KEPT_ROWS = 32
+GPSIMD_ADDS = 5
 HALVES = 2
 JH = J // HALVES
 N_TILES = N // P
@@ -32,17 +36,38 @@ def tile_list_soft_silu_kernel(tc, xT, wgt, w_words, w_scales, iw0, iw1, b, offs
         psum = ctx.enter_context(tc.psum_pool(name="psum", bufs=1))
 
         offsets = keep.tile([P, PICKS * J // LIST_ROWS], U16, name="offsets")
-        wgt_sb = [keep.tile([P, J], F32, name=f"wgt{c}") for c in range(PICKS)]
+        wgt_sb = keep.tile([P, PICKS * J], F32, name="wgt_sb")
+        spread_cols = PICKS * J - JH
+        some_rows = keep.tile([P, spread_cols], F32, name="some_rows")
+        nc.sync.dma_start(some_rows[0:KEPT_ROWS, :], wgt[0 : P : P // KEPT_ROWS, JH:])
+        nc.vector.memset(some_rows[KEPT_ROWS : 2 * KEPT_ROWS, :], 0.0)
+        nc.vector.memset(some_rows[2 * KEPT_ROWS :, :], 0.0)
+        identity = keep.tile([P, P], F32, name="identity")
+        make_identity(nc, identity[:])
         x_planes = xT.rearrange("(p i) t -> i p t", i=PACK)
         x_sb = []
         for i in range(PACK):
-            plane = keep.tile([P, T], F32, name=f"x_plane{i}")
+            plane = keep.tile([P, T], F32, name=f"x_plane{i}", tag=f"x_plane{i}")
             nc.sync.dma_start(plane[:], x_planes[i])
             x_sb.append(plane)
             if i == 0:
                 nc.sync.dma_start(offsets[:], offs)
-                for c in range(PICKS):
-                    nc.sync.dma_start(wgt_sb[c][:], wgt[:, c * J : (c + 1) * J])
+                nc.sync.dma_start(wgt_sb[:, 0:JH], wgt[:, 0:JH])
+
+        blocks = spread_cols // P // 2
+        spread = [(JH + blocks * P, blocks * P), (JH, blocks * P)]
+        for piece, (start, count) in enumerate(spread):
+            turned = psum.tile([P, blocks, P], F32, name=f"turned{piece}", tag=f"bank{2 * piece}")
+            for u in range(blocks):
+                first = start - JH + u * P
+                nc.tensor.transpose(turned[:, u, :], some_rows[:, first : first + P], identity[:])
+            repeated = keep.tile([P, blocks, HEADS, LIST_ROWS], F32, name=f"repeated{piece}")
+            one_a_head = turned[:, :, 0 : KEPT_ROWS : KEPT_ROWS // HEADS]
+            nc.scalar.copy(repeated[:], one_a_head.unsqueeze(3).to_broadcast([P, blocks, HEADS, LIST_ROWS]))
+            back = psum.tile([P, blocks, P], F32, name=f"back{piece}", tag=f"bank{2 * piece + 1}")
+            for u in range(blocks):
+                nc.tensor.transpose(back[:, u, :], repeated[:, u].rearrange("p g r -> p (g r)"), identity[:])
+            nc.scalar.copy(wgt_sb[:, start : start + count], back[:].rearrange("p u j -> p (u j)"))
 
         w_codes = keep.tile([P, N], U32, name="w_codes", align_bytes=64)
         nc.sync.dma_start(w_codes[:].bitcast(I32), w_words[0].rearrange("p n i -> p (n i)").bitcast(I32))
@@ -53,86 +78,91 @@ def tile_list_soft_silu_kernel(tc, xT, wgt, w_words, w_scales, iw0, iw1, b, offs
 
         iw_sb = []
         bias = keep.tile([P, N_TILES], F32, name="bias")
-        for t in range(N_TILES):
-            both = keep.tile([P, PICKS, J], F32, name=f"iw_rows{t}")
+        for h in range(HALVES):
+            both = keep.tile([P, PICKS, N_TILES, JH], F32, name=f"iw_half{h}")
             for c, iw in enumerate((iw0, iw1)):
-                nc.sync.dma_start(both[:, c, :], iw[t * P : (t + 1) * P, :])
+                nc.sync.dma_start(both[:, c], iw[:, h * JH : (h + 1) * JH].rearrange("(t p) j -> p t j", p=P))
             iw_sb.append(both)
-            if t == 1:
-                with nc.allow_non_contiguous_dma(reason="one bias value a partition"):
-                    nc.sync.dma_start(bias[:], b.rearrange("(t p) -> p t", p=P))
+        with nc.allow_non_contiguous_dma(reason="one bias value a partition"):
+            nc.sync.dma_start(bias[:], b.rearrange("(t p) -> p t", p=P))
 
         def gather(dst, i, first, count):
             window = x_sb[i][:].indirect(offsets[:, first // LIST_ROWS : (first + count) // LIST_ROWS])
-            nc.vector.tensor_tensor(dst, window, wgt_sb[first // J][:, first % J : first % J + count], MULT)
+            nc.vector.tensor_tensor(dst, window, wgt_sb[:, first : first + count], MULT)
 
         chunks = [(h, c) for h in range(HALVES) for c in range(PICKS)]
-        low = [keep.tile([P, 2, J], F32, name=f"low{c}") for c in range(PICKS)]
-        high = {hc: keep.tile([P, 2, JH], F32, name=f"high{hc[0]}{hc[1]}") for hc in chunks}
+        low = keep.tile([P, 2, PICKS * J], F32, name="low")
+        high_all = keep.tile([P, len(chunks), 2, JH], F32, name="high_all", tag="x_plane1")
+        high = {hc: high_all[:, u] for u, hc in enumerate(chunks)}
         woven = {hc: keep.tile([P, JH, PACK], BF16, name=f"woven{hc[0]}{hc[1]}", align_bytes=64) for hc in chunks}
-        codes = {hc: keep.tile([P, JH], U32, name=f"codes{hc[0]}{hc[1]}", align_bytes=64) for hc in chunks}
-        scale = {hc: keep.tile([P, JH], U8, name=f"scale{hc[0]}{hc[1]}", align_bytes=64) for hc in chunks}
+        codes = [keep.tile([P, PICKS * JH], U32, name=f"codes{h}", align_bytes=64) for h in range(HALVES)]
+        scale = [keep.tile([P, PICKS * JH], U8, name=f"scale{h}", align_bytes=64) for h in range(HALVES)]
 
-        for i in range(2):
-            for c in range(PICKS):
-                gather(low[c][:, i, :], i, c * J, J)
+        for first, count in [(0, JH)] + spread:
+            gather(low[:, 0, first : first + count], 0, first, count)
         for c in range(PICKS):
+            gather(low[:, 1, c * J : (c + 1) * J], 1, c * J, J)
             for h in range(HALVES):
-                nc.scalar.copy(woven[h, c][:, :, 0:2], low[c][:, :, h * JH : (h + 1) * JH].rearrange("p i j -> p j i"))
-        for i in range(2, PACK):
-            for h, c in chunks:
-                gather(high[h, c][:, i - 2, :], i, c * J + h * JH, JH)
-        for h, c in chunks:
-            nc.scalar.copy(woven[h, c][:, :, 2:4], high[h, c][:].rearrange("p i j -> p j i"))
+                first = c * J + h * JH
+                nc.scalar.copy(woven[h, c][:, :, 0:2], low[:, :, first : first + JH].rearrange("p i j -> p j i"))
 
-        banks = {(h, t): psum.tile([P, PICKS, JH], F32, name=f"bank{h}{t}") for h in range(HALVES) for t in range(N_TILES)}
+        def gather_high(i, some_chunks):
+            for h, c in some_chunks:
+                gather(high[h, c][:, i - 2, :], i, c * J + h * JH, JH)
+                if i == PACK - 1:
+                    nc.scalar.copy(woven[h, c][:, :, 2:4], high[h, c].rearrange("p i j -> p j i"))
+
+        gather_high(2, chunks[:3])
+        gather_high(3, chunks[:2])
+        gather_high(2, chunks[3:])
+        gather_high(3, chunks[2:])
+
+        banks = {(h, t): psum.tile([P, PICKS, JH], F32, name=f"sums{h}{t}", tag=f"bank{h * N_TILES + t}") for h in range(HALVES) for t in range(N_TILES)}
 
         def quantise(h, c):
+            cols = slice(c * JH, (c + 1) * JH)
             nc.vector.quantize_mx(
-                out=codes[h, c][:].bitcast(FP8X4), scales=scale[h, c][:], in_=woven[h, c][:].rearrange("p j i -> p (j i)")
+                out=codes[h][:, cols].bitcast(FP8X4), scales=scale[h][:, cols], in_=woven[h, c][:].rearrange("p j i -> p (j i)")
             )
 
         def project(h, t):
             cols = slice(t * P, (t + 1) * P)
-            for c in range(PICKS):
-                nc.tensor.matmul_mx(
-                    out=banks[h, t][:, c, :],
-                    lhsT=w_codes[:, cols].bitcast(FP8X4),
-                    lhsT_scale=w_scale[:, cols],
-                    rhs=codes[h, c][:].bitcast(FP8X4),
-                    rhs_scale=scale[h, c][:],
-                    start=True,
-                    stop=True,
-                )
+            nc.tensor.matmul_mx(
+                out=banks[h, t][:].rearrange("p c j -> p (c j)"),
+                lhsT=w_codes[:, cols].bitcast(FP8X4),
+                lhsT_scale=w_scale[:, cols],
+                rhs=codes[h][:].bitcast(FP8X4),
+                rhs_scale=scale[h][:],
+                start=True,
+                stop=True,
+            )
 
         def weigh(h, t):
             terms = keep.tile([P, PICKS, JH], F32, name=f"terms{h}{t}")
-            nc.vector.tensor_tensor(terms[:], banks[h, t][:], iw_sb[t][:, :, h * JH : (h + 1) * JH], MULT)
+            nc.vector.tensor_tensor(terms[:], banks[h, t][:], iw_sb[h][:, :, t, :], MULT)
             return terms
 
         def finish(t, pooled, cols, label):
             result = keep.tile(list(pooled.shape), F32, name=f"result{label}")
-            nc.scalar.activation(result[:], pooled[:], SILU, bias=bias[:, t : t + 1])
+            nc.scalar.activation(result[:], pooled, SILU, bias=bias[:, t : t + 1])
             nc.sync.dma_start(out[t * P : (t + 1) * P, cols], result[:])
+
+        units = [(h, t) for h in range(HALVES) for t in range(N_TILES)]
+
+        def pool(h, t, terms, adder):
+            pooled = keep.tile([P, JH], F32, name=f"pooled{h}{t}")
+            adder.tensor_tensor(pooled[:], terms[:, 0, :], terms[:, 1, :], ADD)
+            finish(t, pooled[:], slice(h * JH, (h + 1) * JH), f"{h}{t}")
 
         for h, c in chunks:
             quantise(h, c)
-        early = [(h, t) for h in range(HALVES) for t in range(2)]
-        late = [(h, t) for t in range(2, N_TILES) for h in range(HALVES)]
-        for h, t in early + late:
+        waiting = []
+        for u, (h, t) in enumerate(units):
             project(h, t)
-        pooled_rows = [keep.tile([P, J], F32, name=f"pooled{t}") for t in range(2)]
-        for h, t in early:
             terms = weigh(h, t)
-            nc.gpsimd.tensor_tensor(pooled_rows[t][:, h * JH : (h + 1) * JH], terms[:, 0, :], terms[:, 1, :], ADD)
-            if h == HALVES - 1:
-                finish(t, pooled_rows[t], slice(0, J), f"{t}")
-
-        def pool_late(h, t, terms, adder):
-            pooled = keep.tile([P, JH], F32, name=f"pooled_late{h}{t}")
-            adder.tensor_tensor(pooled[:], terms[:, 0, :], terms[:, 1, :], ADD)
-            finish(t, pooled, slice(h * JH, (h + 1) * JH), f"_late{h}{t}")
-
-        late_terms = [weigh(h, t) for h, t in late]
-        for u, ((h, t), terms) in enumerate(zip(late, late_terms)):
-            pool_late(h, t, terms, nc.gpsimd if u == 0 else nc.vector)
+            if u < GPSIMD_ADDS:
+                pool(h, t, terms, nc.gpsimd)
+            else:
+                waiting.append((h, t, terms))
+        for h, t, terms in waiting:
+            pool(h, t, terms, nc.vector)

from contextlib import ExitStack

import concourse.mybir as mybir
from concourse.masks import make_identity

K, N, T, J = 512, 512, 2048, 512
PICKS = 2
FLOPS = 2 * K * N * J * PICKS

F32 = mybir.dt.float32
BF16 = mybir.dt.bfloat16
I32 = mybir.dt.int32
U32 = mybir.dt.uint32
U16 = mybir.dt.uint16
U8 = mybir.dt.uint8
FP8X4 = mybir.dt.float8_e4m3fn_x4
MULT = mybir.AluOpType.mult
ADD = mybir.AluOpType.add
SILU = mybir.ActivationFunctionType.Silu

P = 128
PACK = 4
LIST_ROWS = 16
HEADS = 8
KEPT_ROWS = 32
GPSIMD_ADDS = 5
HALVES = 2
JH = J // HALVES
N_TILES = N // P


def tile_list_soft_silu_kernel(tc, xT, wgt, w_words, w_scales, iw0, iw1, b, offs, out):
    nc = tc.nc
    with ExitStack() as ctx:
        keep = ctx.enter_context(tc.tile_pool(name="keep", bufs=1))
        psum = ctx.enter_context(tc.psum_pool(name="psum", bufs=1))

        offsets = keep.tile([P, PICKS * J // LIST_ROWS], U16, name="offsets")
        wgt_sb = keep.tile([P, PICKS * J], F32, name="wgt_sb")
        spread_cols = PICKS * J - JH
        some_rows = keep.tile([P, spread_cols], F32, name="some_rows")
        nc.sync.dma_start(some_rows[0:KEPT_ROWS, :], wgt[0 : P : P // KEPT_ROWS, JH:])
        nc.vector.memset(some_rows[KEPT_ROWS : 2 * KEPT_ROWS, :], 0.0)
        nc.vector.memset(some_rows[2 * KEPT_ROWS :, :], 0.0)
        identity = keep.tile([P, P], F32, name="identity")
        make_identity(nc, identity[:])
        x_planes = xT.rearrange("(p i) t -> i p t", i=PACK)
        x_sb = []
        for i in range(PACK):
            plane = keep.tile([P, T], F32, name=f"x_plane{i}", tag=f"x_plane{i}")
            nc.sync.dma_start(plane[:], x_planes[i])
            x_sb.append(plane)
            if i == 0:
                nc.sync.dma_start(offsets[:], offs)
                nc.sync.dma_start(wgt_sb[:, 0:JH], wgt[:, 0:JH])

        blocks = spread_cols // P // 2
        spread = [(JH + blocks * P, blocks * P), (JH, blocks * P)]
        for piece, (start, count) in enumerate(spread):
            turned = psum.tile([P, blocks, P], F32, name=f"turned{piece}", tag=f"bank{2 * piece}")
            for u in range(blocks):
                first = start - JH + u * P
                nc.tensor.transpose(turned[:, u, :], some_rows[:, first : first + P], identity[:])
            repeated = keep.tile([P, blocks, HEADS, LIST_ROWS], F32, name=f"repeated{piece}")
            one_a_head = turned[:, :, 0 : KEPT_ROWS : KEPT_ROWS // HEADS]
            nc.scalar.copy(repeated[:], one_a_head.unsqueeze(3).to_broadcast([P, blocks, HEADS, LIST_ROWS]))
            back = psum.tile([P, blocks, P], F32, name=f"back{piece}", tag=f"bank{2 * piece + 1}")
            for u in range(blocks):
                nc.tensor.transpose(back[:, u, :], repeated[:, u].rearrange("p g r -> p (g r)"), identity[:])
            nc.scalar.copy(wgt_sb[:, start : start + count], back[:].rearrange("p u j -> p (u j)"))

        w_codes = keep.tile([P, N], U32, name="w_codes", align_bytes=64)
        nc.sync.dma_start(w_codes[:].bitcast(I32), w_words[0].rearrange("p n i -> p (n i)").bitcast(I32))
        w_scale = keep.tile([P, N], U8, name="w_scale", align_bytes=64)
        nc.gpsimd.memset(w_scale[:].bitcast(I32), 0)
        for q in range(4):
            nc.sync.dma_start(w_scale[32 * q : 32 * q + 4, :].bitcast(I32), w_scales[0, 4 * q : 4 * q + 4, :].bitcast(I32))

        iw_sb = []
        bias = keep.tile([P, N_TILES], F32, name="bias")
        for h in range(HALVES):
            both = keep.tile([P, PICKS, N_TILES, JH], F32, name=f"iw_half{h}")
            for c, iw in enumerate((iw0, iw1)):
                nc.sync.dma_start(both[:, c], iw[:, h * JH : (h + 1) * JH].rearrange("(t p) j -> p t j", p=P))
            iw_sb.append(both)
        with nc.allow_non_contiguous_dma(reason="one bias value a partition"):
            nc.sync.dma_start(bias[:], b.rearrange("(t p) -> p t", p=P))

        def gather(dst, i, first, count):
            window = x_sb[i][:].indirect(offsets[:, first // LIST_ROWS : (first + count) // LIST_ROWS])
            nc.vector.tensor_tensor(dst, window, wgt_sb[:, first : first + count], MULT)

        chunks = [(h, c) for h in range(HALVES) for c in range(PICKS)]
        low = keep.tile([P, 2, PICKS * J], F32, name="low")
        high_all = keep.tile([P, len(chunks), 2, JH], F32, name="high_all", tag="x_plane1")
        high = {hc: high_all[:, u] for u, hc in enumerate(chunks)}
        woven = {hc: keep.tile([P, JH, PACK], BF16, name=f"woven{hc[0]}{hc[1]}", align_bytes=64) for hc in chunks}
        codes = [keep.tile([P, PICKS * JH], U32, name=f"codes{h}", align_bytes=64) for h in range(HALVES)]
        scale = [keep.tile([P, PICKS * JH], U8, name=f"scale{h}", align_bytes=64) for h in range(HALVES)]

        for first, count in [(0, JH)] + spread:
            gather(low[:, 0, first : first + count], 0, first, count)
        for c in range(PICKS):
            gather(low[:, 1, c * J : (c + 1) * J], 1, c * J, J)
            for h in range(HALVES):
                first = c * J + h * JH
                nc.scalar.copy(woven[h, c][:, :, 0:2], low[:, :, first : first + JH].rearrange("p i j -> p j i"))

        def gather_high(i, some_chunks):
            for h, c in some_chunks:
                gather(high[h, c][:, i - 2, :], i, c * J + h * JH, JH)
                if i == PACK - 1:
                    nc.scalar.copy(woven[h, c][:, :, 2:4], high[h, c].rearrange("p i j -> p j i"))

        gather_high(2, chunks[:3])
        gather_high(3, chunks[:2])
        gather_high(2, chunks[3:])
        gather_high(3, chunks[2:])

        banks = {(h, t): psum.tile([P, PICKS, JH], F32, name=f"sums{h}{t}", tag=f"bank{h * N_TILES + t}") for h in range(HALVES) for t in range(N_TILES)}

        def quantise(h, c):
            cols = slice(c * JH, (c + 1) * JH)
            nc.vector.quantize_mx(
                out=codes[h][:, cols].bitcast(FP8X4), scales=scale[h][:, cols], in_=woven[h, c][:].rearrange("p j i -> p (j i)")
            )

        def project(h, t):
            cols = slice(t * P, (t + 1) * P)
            nc.tensor.matmul_mx(
                out=banks[h, t][:].rearrange("p c j -> p (c j)"),
                lhsT=w_codes[:, cols].bitcast(FP8X4),
                lhsT_scale=w_scale[:, cols],
                rhs=codes[h][:].bitcast(FP8X4),
                rhs_scale=scale[h][:],
                start=True,
                stop=True,
            )

        def weigh(h, t):
            terms = keep.tile([P, PICKS, JH], F32, name=f"terms{h}{t}")
            nc.vector.tensor_tensor(terms[:], banks[h, t][:], iw_sb[h][:, :, t, :], MULT)
            return terms

        def finish(t, pooled, cols, label):
            result = keep.tile(list(pooled.shape), F32, name=f"result{label}")
            nc.scalar.activation(result[:], pooled, SILU, bias=bias[:, t : t + 1])
            nc.sync.dma_start(out[t * P : (t + 1) * P, cols], result[:])

        units = [(h, t) for h in range(HALVES) for t in range(N_TILES)]

        def pool(h, t, terms, adder):
            pooled = keep.tile([P, JH], F32, name=f"pooled{h}{t}")
            adder.tensor_tensor(pooled[:], terms[:, 0, :], terms[:, 1, :], ADD)
            finish(t, pooled[:], slice(h * JH, (h + 1) * JH), f"{h}{t}")

        for h, c in chunks:
            quantise(h, c)
        waiting = []
        for u, (h, t) in enumerate(units):
            project(h, t)
            terms = weigh(h, t)
            if u < GPSIMD_ADDS:
                pool(h, t, terms, nc.gpsimd)
            else:
                waiting.append((h, t, terms))
        for h, t, terms in waiting:
            pool(h, t, terms, nc.vector)
